import numpy as np
import ml_dtypes


def mxq(x, axis, fmt="e4m3"):
    dtype, down = {"e4m3": (ml_dtypes.float8_e4m3fn, 7), "e5m2": (ml_dtypes.float8_e5m2, 14)}[fmt]
    v = np.moveaxis(np.asarray(x, np.float32).astype(ml_dtypes.bfloat16).astype(np.float64), axis, -1)
    blocks = v.reshape(v.shape[:-1] + (-1, 32))
    amax = np.abs(blocks).max(-1, keepdims=True)
    byte = np.maximum(np.where(amax > 0, np.frexp(amax)[1] - 1 + 127, 0) - down, 1)
    scale = np.exp2(byte - 127.0)
    codes = (blocks / scale).astype(np.float32).astype(dtype).astype(np.float64)
    return np.moveaxis((codes * scale).reshape(v.shape), -1, axis)


WIDE = False


def mx_kscale(k):
    if not WIDE:
        return np.ones(k)
    levels = np.array([30, -30])
    if k % 512:
        return np.exp2(np.random.permutation(np.resize(levels, k // 32))).repeat(32)
    a = np.empty((k // 512, 16))
    for p in range(k // 512):
        a[p, :8] = np.random.permutation(np.resize(levels, 8))
        for g in range(8):
            far = levels[np.abs(levels - a[p, g]) >= 10]
            a[p, g + 8] = far[np.random.randint(len(far))]
    return np.exp2(a.ravel()).repeat(32)


def f64(x):
    return np.asarray(x).astype(np.float64)


def striped(idx):
    return np.tile(np.asarray(idx).reshape(-1, 16).T, (8, 1)).astype(np.uint16)


def unstriped(offs):
    return offs[:16].T.reshape(-1).astype(np.int64)


E2M1 = np.array([0.0, 0.5, 1.0, 1.5, 2.0, 3.0, 4.0, 6.0, -0.0, -0.5, -1.0, -1.5, -2.0, -3.0, -4.0, -6.0])


def pack_weight(w, fmt):
    k, n = w.shape
    w = f64(np.asarray(w, np.float32).astype(ml_dtypes.bfloat16)).reshape(k // 32, 32, n)
    amax = np.abs(w).max(1)
    if fmt == "e4m3":
        byte = np.frexp(amax)[1] - 1 + 127 - 7
    else:
        mant, ex = np.frexp(amax / 6.0)
        byte = np.where(mant > 0.5, ex, ex - 1) + 127
    byte = np.clip(np.where(amax > 0, byte, 1), 1, 254)
    scaled = (w * np.exp2(127.0 - byte)[:, None, :]).reshape(k, n).astype(np.float32)
    by_word = np.ascontiguousarray(scaled.reshape(k // 512, 128, 4, n).transpose(0, 1, 3, 2))
    if fmt == "e4m3":
        words = by_word.astype(ml_dtypes.float8_e4m3fn).view(np.uint8)
    else:
        c = by_word.astype(ml_dtypes.float4_e2m1fn).view(np.uint8) & 0xF
        words = (c[..., 0::2] | (c[..., 1::2] << 4)).reshape(k // 512, 128, 2 * n)
    return np.ascontiguousarray(words), np.ascontiguousarray(byte.astype(np.uint8).reshape(k // 512, 16, n))


def unpack_weight(words, scales, fmt):
    g, _, n = scales.shape
    words = np.ascontiguousarray(words).reshape(g, 128, n, -1)
    if fmt == "e4m3":
        vals = words.view(ml_dtypes.float8_e4m3fn).astype(np.float64)
    else:
        nib = np.empty((g, 128, n, 4), np.uint8)
        nib[..., 0::2] = words & 0xF
        nib[..., 1::2] = words >> 4
        vals = E2M1[nib]
    vals = vals * np.repeat(np.exp2(scales.astype(np.float64) - 127.0), 8, axis=1)[..., None]
    return vals.transpose(0, 1, 3, 2).reshape(g * 512, n)


def bf(x):
    return np.asarray(x, np.float32).astype(ml_dtypes.bfloat16)


def planes(Y):
    r, m = Y.shape
    b = f64(bf(Y)).reshape(r // 32, 32, m)
    amax = np.abs(b).max(1)
    byte = np.clip(np.where(amax > 0, np.frexp(amax)[1] - 1 + 127 - 7, 1), 1, 254)
    codes = (b * np.exp2(127.0 - byte)[:, None, :]).reshape(r, m).astype(np.float32).astype(ml_dtypes.float8_e4m3fn).view(np.uint8)
    words = codes.reshape(r // 512, 128, 4, m).transpose(0, 1, 3, 2)
    return np.ascontiguousarray(words), np.ascontiguousarray(byte.astype(np.uint8).reshape(r // 512, 16, m))


N, K, T, J = 1024, 512, 1024, 512


def setup_inputs():
    n = np.random.standard_normal
    idx = np.random.permutation(T)[:J]
    fn = mx_kscale(N)
    wp = pack_weight(n((N, K)) * 1 / np.sqrt(N) * fn[:, None], "e4m3")
    return {
        "g": (n((N, T)) * np.exp(0.5 * n((1, T))) / fn[:, None]).astype(np.float32),
        "sv": (n((N, T))).astype(np.float32),
        "w_words": wp[0],
        "w_scales": wp[1],
        "run": (0.3 * n((K, T))).astype(np.float32),
        "offs": striped(idx),
    }


def reference(g, sv, w_words, w_scales, run, offs):
    idx = unstriped(offs)
    wu = unpack_weight(w_words, w_scales, "e4m3")
    d = 2.0 * f64(g)[:, idx] * np.maximum(f64(sv)[:, idx], 0.0)
    dq = mxq(d, 0, "e5m2")
    p = wu.T @ dq
    pp = np.zeros((K, T))
    pp[:, idx] = p
    y = pp + f64(run)
    words, scales = planes(y)
    return y, words, scales

@@ -1,0 +1,225 @@
+from contextlib import ExitStack
+
+import concourse.mybir as mybir
+from concourse.masks import make_identity
+
+N, K, T, J = 1024, 512, 1024, 512
+FLOPS = 2 * N * K * J
+
+F32 = mybir.dt.float32
+BF16 = mybir.dt.bfloat16
+I32 = mybir.dt.int32
+U32 = mybir.dt.uint32
+U16 = mybir.dt.uint16
+U8 = mybir.dt.uint8
+E4M3 = mybir.dt.float8_e4m3fn_x4
+E5M2 = mybir.dt.float8_e5m2_x4
+MULT = mybir.AluOpType.mult
+ADD = mybir.AluOpType.add
+RELU = mybir.ActivationFunctionType.Relu
+
+P = 128
+PACK = 4
+PASSES = N // (P * PACK)
+BANK = 512
+HALF = J // 2
+
+
+def interleave(copy, dst, src, c0, c1):
+    copy(
+        dst[:].rearrange("p (c i) r -> p c r i", i=4),
+        src[:, :, c0:c1].rearrange("p r (c i) -> p c r i", i=4),
+    )
+
+
+def tile_moe_expert_input_gradient_rectified_pl_kernel(
+    tc, g, sv, w_words, w_scales, run, offs, out_0, out_1, out_2
+):
+    nc = tc.nc
+    with ExitStack() as ctx:
+        keep = ctx.enter_context(tc.tile_pool(name="keep", bufs=1))
+        work = ctx.enter_context(tc.tile_pool(name="work", bufs=3))
+        psum = ctx.enter_context(tc.psum_pool(name="psum", bufs=1))
+
+        offsets = keep.tile([P, J // 16], U16, name="offsets")
+        late = ctx.enter_context(tc.tile_pool(name="late", bufs=1))
+
+        planes = PASSES * PACK
+        g_rows = g.rearrange("(z p r) t -> z r p t", z=PASSES, r=PACK)
+        sv_rows = sv.rearrange("(z p r) t -> z r p t", z=PASSES, r=PACK)
+        run_rows = run.rearrange("(p r) t -> r p t", r=PACK)
+        out_rows = out_0.rearrange("(p r) t -> r p t", r=PACK)
+        g_sb = [keep.tile([P, T], F32, name=f"g{i}") for i in range(planes)]
+        sv_sb = [keep.tile([P, T], F32, name=f"sv{i}") for i in range(planes)]
+        run_sb = [keep.tile([P, T], F32, name=f"run{r}") for r in range(PACK)]
+        pp = [keep.tile([P, T], F32, name=f"pp{r}") for r in range(PACK)]
+        w_raw = keep.tile([P, PASSES, K], U32, name="w_raw")
+        ws_raw = keep.tile([P, PASSES, K], U8, name="ws_raw")
+        ident = keep.tile([P, P], F32, name="ident")
+
+        nc.vector.memset(ws_raw[:].rearrange("p z c -> p (z c)").bitcast(I32), 0)
+        for r in range(PACK):
+            nc.vector.memset(pp[r][:], 0.0)
+        make_identity(nc, ident[:])
+
+        def load_plane(tiles, rows, i):
+            nc.sync.dma_start(tiles[i][:], rows[i // PACK, i % PACK])
+
+        load_plane(sv_sb, sv_rows, 0)
+        nc.sync.dma_start(offsets[:], offs)
+        for i in range(planes):
+            if i + 1 < planes:
+                load_plane(sv_sb, sv_rows, i + 1)
+            load_plane(g_sb, g_rows, i)
+            if i == 2:
+                nc.sync.dma_start(
+                    w_raw[:].bitcast(I32),
+                    w_words.rearrange("z p c r -> p z (c r)").bitcast(I32),
+                )
+                ws_rows = w_scales.rearrange("z (q i) c -> i q z c", i=4)
+                for i4 in range(4):
+                    nc.sync.dma_start(ws_raw[i4:P:32].bitcast(I32), ws_rows[i4].bitcast(I32))
+        for r in range(PACK):
+            nc.sync.dma_start(run_sb[r][:], run_rows[r])
+
+        acc = [psum.tile([P, J], F32, name=f"acc{r}") for r in range(PACK)]
+        d32 = [keep.tile([P, PACK, J], F32, name=f"d32_{z}") for z in range(PASSES)]
+        d_codes = keep.tile([P, PASSES, J], U32, name="d_codes", align_bytes=64)
+        d_scales = keep.tile([P, PASSES, J], U8, name="d_scales", align_bytes=64)
+        rect = {}
+
+        def gather_sv(i):
+            picked = work.tile([P, J], F32, name="picked")
+            nc.vector.tensor_copy(picked[:], sv_sb[i][:].indirect(offsets[:]))
+            rect[i] = work.tile([P, J], F32, name="rect")
+            nc.scalar.activation(rect[i][:], picked[:], RELU, scale=2.0)
+
+        def gather_g(i, c0, c1):
+            z, r = divmod(i, PACK)
+            nc.vector.tensor_tensor(
+                d32[z][:, r, c0:c1],
+                g_sb[i][:].indirect(offsets[:, c0 // 16 : c1 // 16]),
+                rect[i][:, c0:c1],
+                MULT,
+            )
+
+        def round_d(z, c0, c1, copy, d16):
+            interleave(copy, d16, d32[z], c0, c1)
+            return d16
+
+        def quantize_d(z, c0, c1, d16):
+            nc.vector.quantize_mx(
+                out=d_codes[:, z, c0:c1].bitcast(E5M2),
+                scales=d_scales[:, z, c0:c1],
+                in_=d16[:].rearrange("p c r -> p (c r)"),
+            )
+
+        def multiply(z, r, words, scales, slot):
+            nc.tensor.matmul_mx(
+                out=acc[r][:],
+                lhsT=words[:, z, slot, :].bitcast(E4M3),
+                lhsT_scale=scales[:, z, slot, :],
+                rhs=d_codes[:, z, :].bitcast(E5M2),
+                rhs_scale=d_scales[:, z, :],
+                start=(z == 0),
+                stop=(z == PASSES - 1),
+            )
+
+        def deal_weights(words, scales, r0, r1):
+            for dealt, raw in ((words, w_raw), (scales, ws_raw)):
+                nc.vector.tensor_copy(
+                    dealt[:], raw[:].rearrange("p z (m r) -> p z r m", r=PACK)[:, :, r0:r1, :]
+                )
+
+        w_first = keep.tile([P, PASSES, 1, P], U32, name="w_first", align_bytes=64)
+        ws_first = keep.tile([P, PASSES, 1, P], U8, name="ws_first", align_bytes=64)
+        d16_0 = keep.tile([P, J, PACK], BF16, name="d16_0", align_bytes=64)
+        d16_a = keep.tile([P, HALF, PACK], BF16, name="d16_a", align_bytes=64)
+        d16_b = late.tile([P, HALF, PACK], BF16, name="d16_b", align_bytes=64, offset=0)
+
+        gather_sv(0)
+        for i in range(planes):
+            if i + 1 < planes:
+                gather_sv(i + 1)
+            if i + 1 < planes:
+                gather_g(i, 0, J)
+            if i == PACK - 1:
+                round_d(0, 0, J, nc.scalar.copy, d16_0)
+            if i == PACK:
+                deal_weights(w_first, ws_first, 0, 1)
+            if i == PACK + 1:
+                quantize_d(0, 0, J, d16_0)
+                multiply(0, 0, w_first, ws_first, 0)
+        last = planes - 1
+        gather_g(last, 0, HALF)
+        round_d(1, 0, HALF, nc.scalar.copy, d16_a)
+        gather_g(last, HALF, J)
+        round_d(1, HALF, J, nc.vector.tensor_copy, d16_b)
+        quantize_d(1, 0, HALF, d16_a)
+        quantize_d(1, HALF, J, d16_b)
+        multiply(1, 0, w_first, ws_first, 0)
+        ws_rest = late.tile([P, PASSES, PACK - 1, P], U8, name="ws_rest", align_bytes=64, offset=0)
+        w_rest = late.tile([P, PASSES, PACK - 1, P], U32, name="w_rest", align_bytes=64, offset=1024)
+        deal_weights(w_rest, ws_rest, 1, PACK)
+        for r in range(1, PACK):
+            for z in range(PASSES):
+                multiply(z, r, w_rest, ws_rest, r - 1)
+
+        y = keep.tile([P, PACK, T], F32, name="y")
+
+        def add_on_tensor(r):
+            for h in range(T // BANK):
+                turned = psum.tile([P, BANK // P, P], F32, name=f"turned{h}")
+                for b in range(BANK // P):
+                    cols = slice(h * BANK + b * P, h * BANK + (b + 1) * P)
+                    nc.tensor.matmul(turned[:, b, :], run_sb[r][:, cols], ident[:],
+                                     start=True, stop=False, is_transpose=True)
+                    nc.tensor.matmul(turned[:, b, :], pp[r][:, cols], ident[:],
+                                     start=False, stop=True, is_transpose=True)
+                turned_sb = work.tile([P, BANK // P, P], F32, name="turned_sb")
+                nc.scalar.copy(turned_sb[:], turned[:])
+                back = psum.tile([P, BANK // P, P], F32, name=f"back{h}")
+                for b in range(BANK // P):
+                    nc.tensor.transpose(back[:, b, :], turned_sb[:, b, :], ident[:])
+                nc.scalar.copy(y[:, r, h * BANK : (h + 1) * BANK], back[:].rearrange("p b m -> p (b m)"))
+
+        p_sb = []
+        for r in range(PACK):
+            p_sb.append(keep.tile([P, J], F32, name=f"p_sb{r}"))
+            nc.scalar.copy(p_sb[r][:], acc[r][:])
+        for r in range(PACK):
+            nc.vector.tensor_copy(pp[r][:].indirect(offsets[:]), p_sb[r][:])
+            if r < PACK - 1:
+                add_on_tensor(r)
+                nc.sync.dma_start(out_rows[r], y[:, r, :])
+
+        y_codes = keep.tile([P, T], U32, name="y_codes", align_bytes=64)
+        y_scales = keep.tile([P, T], U8, name="y_scales", align_bytes=64)
+        r = PACK - 1
+        chunk = 256
+        chunks = T // chunk
+        for c in range(chunks):
+            cols = slice(c * chunk, (c + 1) * chunk)
+            nc.vector.tensor_tensor(y[:, r, cols], pp[r][:, cols], run_sb[r][:, cols], ADD)
+            if c % 2 == 1:
+                half = slice((c - 1) * chunk, (c + 1) * chunk)
+                nc.sync.dma_start(out_rows[r][:, half], y[:, r, half])
+        y16 = []
+        for c in range(chunks):
+            y16.append(keep.tile([P, chunk, PACK], BF16, name=f"y16_{c}", align_bytes=64))
+            copy = nc.scalar.copy if c < 2 else nc.vector.tensor_copy
+            interleave(copy, y16[c], y, c * chunk, (c + 1) * chunk)
+        words_out = out_1[0].rearrange("p c r -> p (c r)").bitcast(I32)
+        for c in (0, 2, 3, 1):
+            cols = slice(c * chunk, (c + 1) * chunk)
+            nc.vector.quantize_mx(
+                out=y_codes[:, cols].bitcast(E4M3),
+                scales=y_scales[:, cols],
+                in_=y16[c][:].rearrange("p c r -> p (c r)"),
+            )
+            nc.sync.dma_start(words_out[:, cols], y_codes[:, cols].bitcast(I32))
+        for q in range(4):
+            (nc.scalar if q % 2 else nc.sync).dma_start(
+                out_2[0, 4 * q : 4 * q + 4, :].bitcast(I32),
+                y_scales[32 * q : 32 * q + 4, :].bitcast(I32),
+            )

@@ -52,33 +52,33 @@ def tile_moe_expert_input_gradient_rectified_pl_kernel(
         g_sb = [keep.tile([P, T], F32, name=f"g{i}") for i in range(planes)]
         sv_sb = [keep.tile([P, T], F32, name=f"sv{i}") for i in range(planes)]
         run_sb = [keep.tile([P, T], F32, name=f"run{r}") for r in range(PACK)]
-        pp = [keep.tile([P, T], F32, name=f"pp{r}") for r in range(PACK)]
+        pp = [keep.tile([P, T], F32, name=f"pp{r}") for r in range(PACK - 1)]
         w_raw = keep.tile([P, PASSES, K], U32, name="w_raw")
         ws_raw = keep.tile([P, PASSES, K], U8, name="ws_raw")
         ident = keep.tile([P, P], F32, name="ident")
 
-        nc.vector.memset(ws_raw[:].rearrange("p z c -> p (z c)").bitcast(I32), 0)
-        for r in range(PACK):
+        nc.gpsimd.memset(ws_raw[:].rearrange("p z c -> p (z c)").bitcast(I32), 0)
+        for r in range(PACK - 1):
             nc.vector.memset(pp[r][:], 0.0)
         make_identity(nc, ident[:])
 
         def load_plane(tiles, rows, i):
             nc.sync.dma_start(tiles[i][:], rows[i // PACK, i % PACK])
 
+        ws_rows = w_scales.rearrange("z (q i) c -> i q z c", i=4)
+        for i4 in range(4):
+            nc.scalar.dma_start(ws_raw[i4:P:32].bitcast(I32), ws_rows[i4].bitcast(I32))
         load_plane(sv_sb, sv_rows, 0)
         nc.sync.dma_start(offsets[:], offs)
         for i in range(planes):
             if i + 1 < planes:
                 load_plane(sv_sb, sv_rows, i + 1)
             load_plane(g_sb, g_rows, i)
-            if i == 2:
+            if i == planes - 1:
                 nc.sync.dma_start(
                     w_raw[:].bitcast(I32),
                     w_words.rearrange("z p c r -> p z (c r)").bitcast(I32),
                 )
-                ws_rows = w_scales.rearrange("z (q i) c -> i q z c", i=4)
-                for i4 in range(4):
-                    nc.sync.dma_start(ws_raw[i4:P:32].bitcast(I32), ws_rows[i4].bitcast(I32))
         for r in range(PACK):
             nc.sync.dma_start(run_sb[r][:], run_rows[r])
 
@@ -128,14 +128,15 @@ def tile_moe_expert_input_gradient_rectified_pl_kernel(
         def deal_weights(words, scales, r0, r1):
             for dealt, raw in ((words, w_raw), (scales, ws_raw)):
                 nc.vector.tensor_copy(
-                    dealt[:], raw[:].rearrange("p z (m r) -> p z r m", r=PACK)[:, :, r0:r1, :]
+                    dealt[:].rearrange("p z r m -> p z m r"),
+                    raw[:].rearrange("p z (m r) -> p z m r", r=PACK)[:, :, :, r0:r1],
                 )
 
         w_first = keep.tile([P, PASSES, 1, P], U32, name="w_first", align_bytes=64)
         ws_first = keep.tile([P, PASSES, 1, P], U8, name="ws_first", align_bytes=64)
         d16_0 = keep.tile([P, J, PACK], BF16, name="d16_0", align_bytes=64)
         d16_a = keep.tile([P, HALF, PACK], BF16, name="d16_a", align_bytes=64)
-        d16_b = late.tile([P, HALF, PACK], BF16, name="d16_b", align_bytes=64, offset=0)
+        d16_b = late.tile([P, HALF, PACK], BF16, name="d16_b", align_bytes=64, offset=4096)
 
         gather_sv(0)
         for i in range(planes):
@@ -145,53 +146,67 @@ def tile_moe_expert_input_gradient_rectified_pl_kernel(
                 gather_g(i, 0, J)
             if i == PACK - 1:
                 round_d(0, 0, J, nc.scalar.copy, d16_0)
-            if i == PACK:
-                deal_weights(w_first, ws_first, 0, 1)
             if i == PACK + 1:
                 quantize_d(0, 0, J, d16_0)
-                multiply(0, 0, w_first, ws_first, 0)
         last = planes - 1
         gather_g(last, 0, HALF)
         round_d(1, 0, HALF, nc.scalar.copy, d16_a)
         gather_g(last, HALF, J)
         round_d(1, HALF, J, nc.vector.tensor_copy, d16_b)
+        deal_weights(w_first, ws_first, 0, 1)
+        multiply(0, 0, w_first, ws_first, 0)
         quantize_d(1, 0, HALF, d16_a)
         quantize_d(1, HALF, J, d16_b)
         multiply(1, 0, w_first, ws_first, 0)
-        ws_rest = late.tile([P, PASSES, PACK - 1, P], U8, name="ws_rest", align_bytes=64, offset=0)
-        w_rest = late.tile([P, PASSES, PACK - 1, P], U32, name="w_rest", align_bytes=64, offset=1024)
+        ws_rest = late.tile([P, PASSES, PACK - 1, P], U8, name="ws_rest", align_bytes=64, offset=4224)
+        w_rest = late.tile([P, PASSES, PACK - 1, P], U32, name="w_rest", align_bytes=64, offset=5120)
         deal_weights(w_rest, ws_rest, 1, PACK)
+        pp.append(late.tile([P, T], F32, name="pp_last", offset=128))
+        nc.vector.memset(pp[PACK - 1][:], 0.0)
         for r in range(1, PACK):
             for z in range(PASSES):
                 multiply(z, r, w_rest, ws_rest, r - 1)
 
         y = keep.tile([P, PACK, T], F32, name="y")
 
+        blocks = BANK // P
+        halves = T // BANK
+
         def add_on_tensor(r):
-            for h in range(T // BANK):
-                turned = psum.tile([P, BANK // P, P], F32, name=f"turned{h}")
-                for b in range(BANK // P):
-                    cols = slice(h * BANK + b * P, h * BANK + (b + 1) * P)
-                    nc.tensor.matmul(turned[:, b, :], run_sb[r][:, cols], ident[:],
-                                     start=True, stop=False, is_transpose=True)
-                    nc.tensor.matmul(turned[:, b, :], pp[r][:, cols], ident[:],
-                                     start=False, stop=True, is_transpose=True)
-                turned_sb = work.tile([P, BANK // P, P], F32, name="turned_sb")
-                nc.scalar.copy(turned_sb[:], turned[:])
-                back = psum.tile([P, BANK // P, P], F32, name=f"back{h}")
-                for b in range(BANK // P):
-                    nc.tensor.transpose(back[:, b, :], turned_sb[:, b, :], ident[:])
+            tag = "acc" if r % 2 else "turned"
+            turned = [psum.tile([P, blocks, P], F32, name=f"{tag}{h}") for h in range(halves)]
+            for source, opens in ((run_sb[r], True), (pp[r], False)):
+                for h in range(halves):
+                    for b in range(blocks):
+                        col = h * BANK + b * P
+                        nc.tensor.matmul(
+                            turned[h][:, b, :], source[:, col : col + P], ident[:],
+                            start=(opens and b == 0),
+                            stop=(not opens and b == blocks - 1),
+                            is_transpose=True,
+                        )
+            turned_sb = []
+            for h in range(halves):
+                turned_sb.append(work.tile([P, blocks, P], F32, name="turned_sb"))
+                nc.scalar.copy(turned_sb[h][:], turned[h][:])
+            for h in range(halves):
+                back = psum.tile([P, blocks, P], F32, name=f"back{h}")
+                for b in range(blocks):
+                    nc.tensor.transpose(back[:, b, :], turned_sb[h][:, b, :], ident[:])
                 nc.scalar.copy(y[:, r, h * BANK : (h + 1) * BANK], back[:].rearrange("p b m -> p (b m)"))
 
         p_sb = []
+        pieces = [((0, HALF), (HALF, J))] + [((0, J),)] * (PACK - 1)
         for r in range(PACK):
             p_sb.append(keep.tile([P, J], F32, name=f"p_sb{r}"))
-            nc.scalar.copy(p_sb[r][:], acc[r][:])
+            for c0, c1 in pieces[r]:
+                nc.scalar.copy(p_sb[r][:, c0:c1], acc[r][:, c0:c1])
         for r in range(PACK):
-            nc.vector.tensor_copy(pp[r][:].indirect(offsets[:]), p_sb[r][:])
+            for c0, c1 in pieces[r]:
+                nc.vector.tensor_copy(pp[r][:].indirect(offsets[:, c0 // 16 : c1 // 16]), p_sb[r][:, c0:c1])
             if r < PACK - 1:
                 add_on_tensor(r)
-                nc.sync.dma_start(out_rows[r], y[:, r, :])
+                nc.scalar.dma_start(out_rows[r], y[:, r, :])
 
         y_codes = keep.tile([P, T], U32, name="y_codes", align_bytes=64)
         y_scales = keep.tile([P, T], U8, name="y_scales", align_bytes=64)

from contextlib import ExitStack

import concourse.mybir as mybir
from concourse.masks import make_identity

N, K, T, J = 1024, 512, 1024, 512
FLOPS = 2 * N * K * J

F32 = mybir.dt.float32
BF16 = mybir.dt.bfloat16
I32 = mybir.dt.int32
U32 = mybir.dt.uint32
U16 = mybir.dt.uint16
U8 = mybir.dt.uint8
E4M3 = mybir.dt.float8_e4m3fn_x4
E5M2 = mybir.dt.float8_e5m2_x4
MULT = mybir.AluOpType.mult
ADD = mybir.AluOpType.add
RELU = mybir.ActivationFunctionType.Relu

P = 128
PACK = 4
PASSES = N // (P * PACK)
BANK = 512
HALF = J // 2


def interleave(copy, dst, src, c0, c1):
    copy(
        dst[:].rearrange("p (c i) r -> p c r i", i=4),
        src[:, :, c0:c1].rearrange("p r (c i) -> p c r i", i=4),
    )


def tile_moe_expert_input_gradient_rectified_pl_kernel(
    tc, g, sv, w_words, w_scales, run, offs, out_0, out_1, out_2
):
    nc = tc.nc
    with ExitStack() as ctx:
        keep = ctx.enter_context(tc.tile_pool(name="keep", bufs=1))
        work = ctx.enter_context(tc.tile_pool(name="work", bufs=3))
        psum = ctx.enter_context(tc.psum_pool(name="psum", bufs=1))

        offsets = keep.tile([P, J // 16], U16, name="offsets")
        late = ctx.enter_context(tc.tile_pool(name="late", bufs=1))

        planes = PASSES * PACK
        g_rows = g.rearrange("(z p r) t -> z r p t", z=PASSES, r=PACK)
        sv_rows = sv.rearrange("(z p r) t -> z r p t", z=PASSES, r=PACK)
        run_rows = run.rearrange("(p r) t -> r p t", r=PACK)
        out_rows = out_0.rearrange("(p r) t -> r p t", r=PACK)
        g_sb = [keep.tile([P, T], F32, name=f"g{i}") for i in range(planes)]
        sv_sb = [keep.tile([P, T], F32, name=f"sv{i}") for i in range(planes)]
        run_sb = [keep.tile([P, T], F32, name=f"run{r}") for r in range(PACK)]
        pp = [keep.tile([P, T], F32, name=f"pp{r}") for r in range(PACK - 1)]
        w_raw = keep.tile([P, PASSES, K], U32, name="w_raw")
        ws_raw = keep.tile([P, PASSES, K], U8, name="ws_raw")
        ident = keep.tile([P, P], F32, name="ident")

        nc.gpsimd.memset(ws_raw[:].rearrange("p z c -> p (z c)").bitcast(I32), 0)
        for r in range(PACK - 1):
            nc.vector.memset(pp[r][:], 0.0)
        make_identity(nc, ident[:])

        def load_plane(tiles, rows, i):
            nc.sync.dma_start(tiles[i][:], rows[i // PACK, i % PACK])

        ws_rows = w_scales.rearrange("z (q i) c -> i q z c", i=4)
        for i4 in range(4):
            nc.scalar.dma_start(ws_raw[i4:P:32].bitcast(I32), ws_rows[i4].bitcast(I32))
        load_plane(sv_sb, sv_rows, 0)
        nc.sync.dma_start(offsets[:], offs)
        for i in range(planes):
            if i + 1 < planes:
                load_plane(sv_sb, sv_rows, i + 1)
            load_plane(g_sb, g_rows, i)
            if i == planes - 1:
                nc.sync.dma_start(
                    w_raw[:].bitcast(I32),
                    w_words.rearrange("z p c r -> p z (c r)").bitcast(I32),
                )
        for r in range(PACK):
            nc.sync.dma_start(run_sb[r][:], run_rows[r])

        acc = [psum.tile([P, J], F32, name=f"acc{r}") for r in range(PACK)]
        d32 = [keep.tile([P, PACK, J], F32, name=f"d32_{z}") for z in range(PASSES)]
        d_codes = keep.tile([P, PASSES, J], U32, name="d_codes", align_bytes=64)
        d_scales = keep.tile([P, PASSES, J], U8, name="d_scales", align_bytes=64)
        rect = {}

        def gather_sv(i):
            picked = work.tile([P, J], F32, name="picked")
            nc.vector.tensor_copy(picked[:], sv_sb[i][:].indirect(offsets[:]))
            rect[i] = work.tile([P, J], F32, name="rect")
            nc.scalar.activation(rect[i][:], picked[:], RELU, scale=2.0)

        def gather_g(i, c0, c1):
            z, r = divmod(i, PACK)
            nc.vector.tensor_tensor(
                d32[z][:, r, c0:c1],
                g_sb[i][:].indirect(offsets[:, c0 // 16 : c1 // 16]),
                rect[i][:, c0:c1],
                MULT,
            )

        def round_d(z, c0, c1, copy, d16):
            interleave(copy, d16, d32[z], c0, c1)
            return d16

        def quantize_d(z, c0, c1, d16):
            nc.vector.quantize_mx(
                out=d_codes[:, z, c0:c1].bitcast(E5M2),
                scales=d_scales[:, z, c0:c1],
                in_=d16[:].rearrange("p c r -> p (c r)"),
            )

        def multiply(z, r, words, scales, slot):
            nc.tensor.matmul_mx(
                out=acc[r][:],
                lhsT=words[:, z, slot, :].bitcast(E4M3),
                lhsT_scale=scales[:, z, slot, :],
                rhs=d_codes[:, z, :].bitcast(E5M2),
                rhs_scale=d_scales[:, z, :],
                start=(z == 0),
                stop=(z == PASSES - 1),
            )

        def deal_weights(words, scales, r0, r1):
            for dealt, raw in ((words, w_raw), (scales, ws_raw)):
                nc.vector.tensor_copy(
                    dealt[:].rearrange("p z r m -> p z m r"),
                    raw[:].rearrange("p z (m r) -> p z m r", r=PACK)[:, :, :, r0:r1],
                )

        w_first = keep.tile([P, PASSES, 1, P], U32, name="w_first", align_bytes=64)
        ws_first = keep.tile([P, PASSES, 1, P], U8, name="ws_first", align_bytes=64)
        d16_0 = keep.tile([P, J, PACK], BF16, name="d16_0", align_bytes=64)
        d16_a = keep.tile([P, HALF, PACK], BF16, name="d16_a", align_bytes=64)
        d16_b = late.tile([P, HALF, PACK], BF16, name="d16_b", align_bytes=64, offset=4096)

        gather_sv(0)
        for i in range(planes):
            if i + 1 < planes:
                gather_sv(i + 1)
            if i + 1 < planes:
                gather_g(i, 0, J)
            if i == PACK - 1:
                round_d(0, 0, J, nc.scalar.copy, d16_0)
            if i == PACK + 1:
                quantize_d(0, 0, J, d16_0)
        last = planes - 1
        gather_g(last, 0, HALF)
        round_d(1, 0, HALF, nc.scalar.copy, d16_a)
        gather_g(last, HALF, J)
        round_d(1, HALF, J, nc.vector.tensor_copy, d16_b)
        deal_weights(w_first, ws_first, 0, 1)
        multiply(0, 0, w_first, ws_first, 0)
        quantize_d(1, 0, HALF, d16_a)
        quantize_d(1, HALF, J, d16_b)
        multiply(1, 0, w_first, ws_first, 0)
        ws_rest = late.tile([P, PASSES, PACK - 1, P], U8, name="ws_rest", align_bytes=64, offset=4224)
        w_rest = late.tile([P, PASSES, PACK - 1, P], U32, name="w_rest", align_bytes=64, offset=5120)
        deal_weights(w_rest, ws_rest, 1, PACK)
        pp.append(late.tile([P, T], F32, name="pp_last", offset=128))
        nc.vector.memset(pp[PACK - 1][:], 0.0)
        for r in range(1, PACK):
            for z in range(PASSES):
                multiply(z, r, w_rest, ws_rest, r - 1)

        y = keep.tile([P, PACK, T], F32, name="y")

        blocks = BANK // P
        halves = T // BANK

        def add_on_tensor(r):
            tag = "acc" if r % 2 else "turned"
            turned = [psum.tile([P, blocks, P], F32, name=f"{tag}{h}") for h in range(halves)]
            for source, opens in ((run_sb[r], True), (pp[r], False)):
                for h in range(halves):
                    for b in range(blocks):
                        col = h * BANK + b * P
                        nc.tensor.matmul(
                            turned[h][:, b, :], source[:, col : col + P], ident[:],
                            start=(opens and b == 0),
                            stop=(not opens and b == blocks - 1),
                            is_transpose=True,
                        )
            turned_sb = []
            for h in range(halves):
                turned_sb.append(work.tile([P, blocks, P], F32, name="turned_sb"))
                nc.scalar.copy(turned_sb[h][:], turned[h][:])
            for h in range(halves):
                back = psum.tile([P, blocks, P], F32, name=f"back{h}")
                for b in range(blocks):
                    nc.tensor.transpose(back[:, b, :], turned_sb[h][:, b, :], ident[:])
                nc.scalar.copy(y[:, r, h * BANK : (h + 1) * BANK], back[:].rearrange("p b m -> p (b m)"))

        p_sb = []
        pieces = [((0, HALF), (HALF, J))] + [((0, J),)] * (PACK - 1)
        for r in range(PACK):
            p_sb.append(keep.tile([P, J], F32, name=f"p_sb{r}"))
            for c0, c1 in pieces[r]:
                nc.scalar.copy(p_sb[r][:, c0:c1], acc[r][:, c0:c1])
        for r in range(PACK):
            for c0, c1 in pieces[r]:
                nc.vector.tensor_copy(pp[r][:].indirect(offsets[:, c0 // 16 : c1 // 16]), p_sb[r][:, c0:c1])
            if r < PACK - 1:
                add_on_tensor(r)
                nc.scalar.dma_start(out_rows[r], y[:, r, :])

        y_codes = keep.tile([P, T], U32, name="y_codes", align_bytes=64)
        y_scales = keep.tile([P, T], U8, name="y_scales", align_bytes=64)
        r = PACK - 1
        chunk = 256
        chunks = T // chunk
        for c in range(chunks):
            cols = slice(c * chunk, (c + 1) * chunk)
            nc.vector.tensor_tensor(y[:, r, cols], pp[r][:, cols], run_sb[r][:, cols], ADD)
            if c % 2 == 1:
                half = slice((c - 1) * chunk, (c + 1) * chunk)
                nc.sync.dma_start(out_rows[r][:, half], y[:, r, half])
        y16 = []
        for c in range(chunks):
            y16.append(keep.tile([P, chunk, PACK], BF16, name=f"y16_{c}", align_bytes=64))
            copy = nc.scalar.copy if c < 2 else nc.vector.tensor_copy
            interleave(copy, y16[c], y, c * chunk, (c + 1) * chunk)
        words_out = out_1[0].rearrange("p c r -> p (c r)").bitcast(I32)
        for c in (0, 2, 3, 1):
            cols = slice(c * chunk, (c + 1) * chunk)
            nc.vector.quantize_mx(
                out=y_codes[:, cols].bitcast(E4M3),
                scales=y_scales[:, cols],
                in_=y16[c][:].rearrange("p c r -> p (c r)"),
            )
            nc.sync.dma_start(words_out[:, cols], y_codes[:, cols].bitcast(I32))
        for q in range(4):
            (nc.scalar if q % 2 else nc.sync).dma_start(
                out_2[0, 4 * q : 4 * q + 4, :].bitcast(I32),
                y_scales[32 * q : 32 * q + 4, :].bitcast(I32),
            )
